import numpy as np
import ml_dtypes


def mxq(x, axis, fmt="e4m3"):
    dtype, down = {"e4m3": (ml_dtypes.float8_e4m3fn, 7), "e5m2": (ml_dtypes.float8_e5m2, 14)}[fmt]
    v = np.moveaxis(np.asarray(x, np.float32).astype(ml_dtypes.bfloat16).astype(np.float64), axis, -1)
    blocks = v.reshape(v.shape[:-1] + (-1, 32))
    amax = np.abs(blocks).max(-1, keepdims=True)
    byte = np.maximum(np.where(amax > 0, np.frexp(amax)[1] - 1 + 127, 0) - down, 1)
    scale = np.exp2(byte - 127.0)
    codes = (blocks / scale).astype(np.float32).astype(dtype).astype(np.float64)
    return np.moveaxis((codes * scale).reshape(v.shape), -1, axis)


WIDE = False


def mx_kscale(k):
    if not WIDE:
        return np.ones(k)
    levels = np.array([10, -10, 5, -5, 0])
    if k % 512:
        return np.exp2(np.random.permutation(np.resize(levels, k // 32))).repeat(32)
    a = np.empty((k // 512, 16))
    for p in range(k // 512):
        a[p, :8] = np.random.permutation(np.resize(levels, 8))
        for g in range(8):
            far = levels[np.abs(levels - a[p, g]) >= 10]
            a[p, g + 8] = far[np.random.randint(len(far))]
    return np.exp2(a.ravel()).repeat(32)


def f64(x):
    return np.asarray(x).astype(np.float64)


def striped(idx):
    return np.tile(idx.reshape(-1, 16).T, (8, 1)).astype(np.uint16)


def unstriped(offs):
    return offs[:16].T.reshape(-1).astype(np.int64)


def striped8(idx):
    return np.concatenate([x.reshape(-1, 16).T for x in idx]).astype(np.uint16)


def runs(offs, k):
    lists = np.stack([offs[16 * r : 16 * r + 16].T.reshape(-1) for r in range(8)]).astype(np.int64)
    return lists[np.arange(k) % 512 // 64]


def pack_weight(w):
    k, n = w.shape
    w = f64(np.asarray(w, np.float32).astype(ml_dtypes.bfloat16)).reshape(k // 32, 32, n)
    amax = np.abs(w).max(1)
    byte = np.clip(np.where(amax > 0, np.frexp(amax)[1] - 1 + 127 - 7, 1), 1, 254)
    scaled = (w * np.exp2(127.0 - byte)[:, None, :]).reshape(k, n).astype(np.float32)
    words = np.ascontiguousarray(scaled.reshape(k // 512, 128, 4, n).transpose(0, 1, 3, 2)).astype(ml_dtypes.float8_e4m3fn).view(np.uint8)
    return words, np.ascontiguousarray(byte.astype(np.uint8).reshape(k // 512, 16, n))


def unpack_weight(words, scales):
    g, p, n, _ = words.shape
    vals = np.ascontiguousarray(words).view(ml_dtypes.float8_e4m3fn).astype(np.float64) * np.repeat(np.exp2(scales.astype(np.float64) - 127.0), 8, axis=1)[..., None]
    return vals.transpose(0, 1, 3, 2).reshape(g * 512, n)


E2M1 = np.array([0.0, 0.5, 1.0, 1.5, 2.0, 3.0, 4.0, 6.0, -0.0, -0.5, -1.0, -1.5, -2.0, -3.0, -4.0, -6.0])


def pack_fp4(w):
    k, n = w.shape
    w = f64(np.asarray(w, np.float32).astype(ml_dtypes.bfloat16)).reshape(k // 32, 32, n)
    amax = np.abs(w).max(1)
    mant, ex = np.frexp(amax / 6.0)
    byte = np.clip(np.where(amax > 0, np.where(mant > 0.5, ex, ex - 1) + 127, 1), 1, 254)
    scaled = (w * np.exp2(127.0 - byte)[:, None, :]).reshape(k, n).astype(np.float32)
    c = np.ascontiguousarray(scaled.reshape(k // 512, 128, 4, n).transpose(0, 1, 3, 2)).astype(ml_dtypes.float4_e2m1fn).view(np.uint8) & 0xF
    words = (c[..., 0::2] | (c[..., 1::2] << 4)).reshape(k // 512, 128, 2 * n)
    return np.ascontiguousarray(words), np.ascontiguousarray(byte.astype(np.uint8).reshape(k // 512, 16, n))


def unpack_fp4(words, scales):
    g, _, n = scales.shape
    words = np.ascontiguousarray(words).reshape(g, 128, n, 2)
    nib = np.empty((g, 128, n, 4), np.uint8)
    nib[..., 0::2] = words & 0xF
    nib[..., 1::2] = words >> 4
    vals = E2M1[nib] * np.repeat(np.exp2(scales.astype(np.float64) - 127.0), 8, axis=1)[..., None]
    return vals.transpose(0, 1, 3, 2).reshape(g * 512, n)


K, T, S, H, G, U = 512, 2048, 256, 512, 2048, 512


def setup_inputs():
    n = np.random.standard_normal
    s = mx_kscale(K)[:, None]
    packed_xT = pack_weight(n((K, T)) * s)
    packed_w1 = pack_fp4(n((K, H)) / np.sqrt(K) / s)
    packed_dT = pack_weight(n((K, G)) / s)
    perm = np.random.permutation(U)
    return {
        "x_words": packed_xT[0],
        "x_scales": packed_xT[1],
        "w1_words": packed_w1[0],
        "w1_scales": packed_w1[1],
        "gs": (np.random.uniform(0.5, 1.5, (K, 1)) * s).astype(np.float32),
        "d_words": packed_dT[0],
        "d_scales": packed_dT[1],
        "offs": striped(np.random.permutation(T)[:S]),
        "n1": striped8(np.stack([np.random.permutation(S) for _ in range(8)])),
        "n2": striped8(np.stack([np.random.permutation(S) for _ in range(8)])),
        "ka": striped8(np.random.randint(0, G, (8, H))),
        "kb": striped8(np.random.randint(0, G, (8, H))),
        "n3": striped(perm[:S]),
        "n4": striped(perm[S:]),
        "n5": striped(np.random.permutation(U)),
    }


def reference(x_words, x_scales, w1_words, w1_scales, gs, d_words, d_scales, offs, n1, n2, ka, kb, n3, n4, n5):
    d_ka = unpack_weight(d_words, d_scales)[np.arange(K)[:, None], runs(ka, K)]
    xq = unpack_weight(x_words, x_scales)[:, unstriped(offs)]
    y = unpack_fp4(w1_words, w1_scales).T @ xq
    z = f64(gs) * (y - (np.minimum(y[np.arange(H)[:, None], runs(n1, H)], y[np.arange(H)[:, None], runs(n2, H)])))
    zq = mxq(z, 0, "e4m3")
    d_kb = unpack_weight(d_words, d_scales)[np.arange(K)[:, None], runs(kb, K)]
    h = 0.0625 * (d_ka.T @ zq + d_kb.T @ zq)
    nw = 0.5 * h
    ph = np.zeros((H, U))
    ph[:, unstriped(n3)] = h
    pg = ph.copy()
    pg[:, unstriped(n4)] = nw
    return pg - pg[:, unstriped(n5)]

@@ -1,0 +1,213 @@
+from contextlib import ExitStack
+
+import concourse.mybir as mybir
+
+K, T, S, H, G, U = 512, 2048, 256, 512, 2048, 512
+FLOPS = 2 * K * H * S * 3
+
+F32 = mybir.dt.float32
+BF16 = mybir.dt.bfloat16
+I32 = mybir.dt.int32
+U32 = mybir.dt.uint32
+U16 = mybir.dt.uint16
+U8 = mybir.dt.uint8
+FP8X4 = mybir.dt.float8_e4m3fn_x4
+FP4X4 = mybir.dt.float4_e2m1fn_x4
+ALU = mybir.AluOpType
+COPY = mybir.ActivationFunctionType.Copy
+
+P = 128
+PACK = 4
+HALF = S // 2
+PAIR = 2 * P
+
+
+def entries(offsets, first, count):
+    return offsets[:, first // 16 : (first + count) // 16]
+
+
+def tile_picked_daqunderpagtwo_none_p_kernel(
+    tc, x_words, x_scales, w1_words, w1_scales, gs, d_words, d_scales, offs, n1, n2, ka, kb, n3, n4, n5, out
+):
+    nc = tc.nc
+    with ExitStack() as ctx:
+        lists = ctx.enter_context(tc.tile_pool(name="lists", bufs=1))
+        keep = ctx.enter_context(tc.tile_pool(name="keep", bufs=1))
+        psum = ctx.enter_context(tc.psum_pool(name="psum", bufs=1))
+
+        def list_tile(source, name):
+            tile = lists.tile([P, source.shape[1]], U16, name=name)
+            nc.sync.dma_start(tile[:], source)
+            return tile
+
+        def load_scale_rows(queue, tile, rows, q):
+            words = rows[4 * q : 4 * q + 4, :].bitcast(I32)
+            queue.dma_start(
+                tile[32 * q : 32 * q + 32, :].bitcast(I32),
+                words.unsqueeze(0).broadcast_to([8, 4, words.shape[1]]),
+            )
+
+        xs_table = keep.tile([P, T], U8, name="xs_table", align_bytes=64)
+        ws_raw = keep.tile([P, H], U8, name="ws_raw", align_bytes=64)
+        ds_table = keep.tile([P, G], U8, name="ds_table", align_bytes=64)
+        nc.vector.memset(ds_table[:].bitcast(I32), 0)
+
+        ww_raw = keep.tile([P, 2 * H], U8, name="ww_raw", align_bytes=64)
+        nc.gpsimd.dma_start(ds_table[0:P:8, :].bitcast(I32), d_scales[0].bitcast(I32))
+        nc.gpsimd.dma_start(ww_raw[:].bitcast(I32), w1_words[0].bitcast(I32))
+        gs_t = keep.tile([P, PACK], F32, name="gs_t")
+        nc.gpsimd.dma_start(gs_t[:], gs.rearrange("(p t) o -> p (t o)", t=PACK))
+
+        offs_t = list_tile(offs, "offs_t")
+        ka_t = list_tile(ka, "ka_t")
+        kb_t = list_tile(kb, "kb_t")
+        for q in range(4):
+            load_scale_rows(nc.scalar if q < 3 else nc.sync, xs_table, x_scales[0], q)
+        xw_table = keep.tile([P, T], U32, name="xw_table", tag="xw_table", align_bytes=64)
+        nc.scalar.dma_start(xw_table[:].bitcast(I32), x_words[0].rearrange("p n t -> p (n t)").bitcast(I32))
+        dw_table = keep.tile([P, G], U32, name="dw_table", align_bytes=64)
+        nc.scalar.dma_start(dw_table[:].bitcast(I32), d_words[0].rearrange("p n t -> p (n t)").bitcast(I32))
+        for q in range(4):
+            load_scale_rows(nc.sync, ws_raw, w1_scales[0], q)
+        n1_t = list_tile(n1, "n1_t")
+        n2_t = list_tile(n2, "n2_t")
+        n3_t = list_tile(n3, "n3_t")
+        n4_t = list_tile(n4, "n4_t")
+        n5_t = list_tile(n5, "n5_t")
+
+        xs = keep.tile([P, S], U8, name="xs", align_bytes=64)
+        nc.vector.tensor_copy(xs[:], xs_table[:].indirect(offs_t[:]))
+
+        ww = keep.tile([P, 2 * H], U8, name="ww", align_bytes=64)
+        nc.scalar.copy(
+            ww[:].bitcast(U16).rearrange("p (t m) -> p t m", t=PACK),
+            ww_raw[:].bitcast(U16).rearrange("p (m t) -> p t m", t=PACK),
+        )
+        ws = keep.tile([P, H], U8, name="ws", align_bytes=64)
+        nc.vector.tensor_copy(
+            ws[:].rearrange("p (t m) -> p t m", t=PACK), ws_raw[:].rearrange("p (m t) -> p t m", t=PACK)
+        )
+
+        def dictionary_scales(pair, picked_tag, placed_tag):
+            picked = keep.tile([P, 2 * PAIR], U8, name=f"ds_picked{pair}", tag=picked_tag, align_bytes=64)
+            for side, codes in enumerate((ka_t, kb_t)):
+                nc.vector.tensor_copy(
+                    picked[:, side * PAIR : (side + 1) * PAIR],
+                    ds_table[:].indirect(entries(codes, pair * PAIR, PAIR)),
+                )
+            placed = keep.tile([P, 2 * PAIR], U8, name=f"ds_placed{pair}", tag=placed_tag, align_bytes=64)
+            nc.vector.memset(placed[:].bitcast(I32), 0)
+            for r in range(4):
+                nc.sync.dma_start(placed[r:P:32, :].bitcast(I32), picked[8 * r : P : 32, :].bitcast(I32))
+            return placed
+
+        def dictionary_words(pair):
+            picked = keep.tile([P, 2 * PAIR], U32, name=f"dw_picked{pair}", tag="dw_picked", align_bytes=64)
+            for side, codes in enumerate((ka_t, kb_t)):
+                nc.vector.tensor_copy(
+                    picked[:, side * PAIR : (side + 1) * PAIR],
+                    dw_table[:].indirect(entries(codes, pair * PAIR, PAIR)),
+                )
+            return picked
+
+        ds0 = dictionary_scales(0, "ds_a", "ds_b")
+        xw = keep.tile([P, S], U32, name="xw", tag="dw_picked", align_bytes=64)
+        nc.vector.tensor_copy(xw[:], xw_table[:].indirect(offs_t[:]))
+
+
+        neg_gs = keep.tile([P, PACK], F32, name="neg_gs")
+        nc.vector.tensor_scalar(neg_gs[:], gs_t[:], -1.0, None, ALU.mult)
+
+        y = []
+        for t in range(PACK):
+            acc = psum.tile([P, S], F32, name=f"y_acc{t}", tag=f"bank{t}")
+            nc.tensor.matmul_mx(
+                out=acc[:],
+                lhsT=ww[:, 2 * P * t : 2 * P * (t + 1)].bitcast(FP4X4),
+                lhsT_scale=ws[:, P * t : P * (t + 1)],
+                rhs=xw[:].bitcast(FP8X4),
+                rhs_scale=xs[:],
+                start=True,
+                stop=True,
+            )
+            y_t = keep.tile([P, S], F32, name=f"y{t}")
+            if t == 0:
+                nc.scalar.activation(y_t[:], acc[:], COPY)
+            else:
+                nc.vector.tensor_copy(y_t[:], acc[:])
+            y.append(y_t)
+
+        z_codes = keep.tile([P, S], U32, name="z_codes", tag="z_codes", align_bytes=64)
+        z_scales = keep.tile([P, S], U8, name="z_scales", align_bytes=64)
+
+        def neighbour_step(half, least_tag):
+            cols = slice(half * HALF, (half + 1) * HALF)
+            z = keep.tile([P, PACK, HALF], F32, name=f"z{half}")
+            work = keep.tile([P, 2 * PACK, HALF], F32, name=f"work{half}", tag=least_tag, align_bytes=64)
+            least, gy = work[:, :PACK, :], work[:, PACK:, :]
+            for t in range(PACK):
+                at1 = keep.tile([P, HALF], F32, name=f"at1_{half}_{t}")
+                at2 = keep.tile([P, HALF], F32, name=f"at2_{half}_{t}")
+                nc.scalar.activation(at1[:], y[t][:].indirect(entries(n1_t, half * HALF, HALF)), COPY)
+                nc.scalar.activation(at2[:], y[t][:].indirect(entries(n2_t, half * HALF, HALF)), COPY)
+                nc.vector.tensor_scalar(gy[:, t, :], y[t][:, cols], gs_t[:, t : t + 1], None, ALU.mult)
+                nc.vector.tensor_tensor(least[:, t, :], at1[:], at2[:], ALU.min)
+                nc.vector.scalar_tensor_tensor(
+                    z[:, t, :], least[:, t, :], neg_gs[:, t : t + 1], gy[:, t, :], ALU.mult, ALU.add
+                )
+            woven = keep.tile([P, HALF * PACK], BF16, name=f"woven{half}", tag=f"woven{half}", align_bytes=64)
+            nc.vector.tensor_copy(
+                woven[:].rearrange("p (c i t) -> p c t i", i=4, t=PACK),
+                z[:].rearrange("p t (c i) -> p c t i", i=4),
+            )
+            nc.vector.quantize_mx(out=z_codes[:, cols].bitcast(FP8X4), scales=z_scales[:, cols], in_=woven[:])
+
+        def second_product(words, scales, block, first, count, bank):
+            acc = psum.tile([P, count], F32, name=f"h_acc{block}_{first}", tag=f"bank{bank}")
+            for side in range(2):
+                c0 = side * PAIR + (block % 2) * P
+                nc.tensor.matmul_mx(
+                    out=acc[:],
+                    lhsT=words[:, c0 : c0 + P].bitcast(FP8X4),
+                    lhsT_scale=scales[:, c0 : c0 + P],
+                    rhs=z_codes[:, first : first + count].bitcast(FP8X4),
+                    rhs_scale=z_scales[:, first : first + count],
+                    start=(side == 0),
+                    stop=(side == 1),
+                )
+            h = keep.tile([P, count], F32, name=f"h{block}_{first}")
+            nc.vector.tensor_scalar(h[:], acc[:], 0.0625, None, ALU.mult)
+            return h
+
+        pages = [keep.tile([P, U], F32, name=f"page{b}") for b in range(H // P)]
+
+        def put(blocks, values, first, count):
+            for b, h in zip(blocks, values):
+                nc.scalar.activation(pages[b][:].indirect(entries(n3_t, first, count)), h[:], COPY)
+            for b, h in zip(blocks, values):
+                nc.scalar.activation(pages[b][:].indirect(entries(n4_t, first, count)), h[:], COPY, scale=0.5)
+
+        def take(b, tag):
+            other = keep.tile([P, U], F32, name=f"other{b}", tag=tag, align_bytes=64)
+            result = keep.tile([P, U], F32, name=f"result{b}")
+            for c0 in range(0, U, S):
+                cols = slice(c0, c0 + S)
+                nc.scalar.activation(other[:, cols], pages[b][:].indirect(entries(n5_t, c0, S)), COPY)
+                nc.vector.tensor_tensor(result[:, cols], pages[b][:, cols], other[:, cols], ALU.subtract)
+                nc.sync.dma_start(out[b * P : (b + 1) * P, cols], result[:, cols])
+
+        dw0 = dictionary_words(0)
+        neighbour_step(0, "least0")
+        first_h = [second_product(dw0, ds0, b, 0, HALF, 4 + b) for b in (0, 1)]
+        neighbour_step(1, "woven0")
+        put((0, 1), first_h, 0, HALF)
+        second_h = [second_product(dw0, ds0, b, HALF, HALF, 6 + b) for b in (0, 1)]
+        put((0, 1), second_h, HALF, HALF)
+        ds1 = dictionary_scales(1, "woven1", "ds_c")
+        dw1 = dictionary_words(1)
+        last_h = [second_product(dw1, ds1, b, 0, S, b) for b in (2, 3)]
+        take(0, "dw_picked")
+        take(1, "z_codes")
+        put((2, 3), last_h, 0, S)
+        take(2, "other2")
+        take(3, "other3")

@@ -40,50 +40,43 @@ def tile_picked_daqunderpagtwo_none_p_kernel(
             nc.sync.dma_start(tile[:], source)
             return tile
 
-        def load_scale_rows(queue, tile, rows, q):
-            words = rows[4 * q : 4 * q + 4, :].bitcast(I32)
-            queue.dma_start(
-                tile[32 * q : 32 * q + 32, :].bitcast(I32),
-                words.unsqueeze(0).broadcast_to([8, 4, words.shape[1]]),
-            )
-
         xs_table = keep.tile([P, T], U8, name="xs_table", align_bytes=64)
         ws_raw = keep.tile([P, H], U8, name="ws_raw", align_bytes=64)
         ds_table = keep.tile([P, G], U8, name="ds_table", align_bytes=64)
         nc.vector.memset(ds_table[:].bitcast(I32), 0)
+        nc.vector.memset(xs_table[:].bitcast(I32), 0)
 
         ww_raw = keep.tile([P, 2 * H], U8, name="ww_raw", align_bytes=64)
-        nc.gpsimd.dma_start(ds_table[0:P:8, :].bitcast(I32), d_scales[0].bitcast(I32))
         nc.gpsimd.dma_start(ww_raw[:].bitcast(I32), w1_words[0].bitcast(I32))
+        nc.gpsimd.dma_start(ds_table[0:P:8, :].bitcast(I32), d_scales[0].bitcast(I32))
         gs_t = keep.tile([P, PACK], F32, name="gs_t")
         nc.gpsimd.dma_start(gs_t[:], gs.rearrange("(p t) o -> p (t o)", t=PACK))
 
         offs_t = list_tile(offs, "offs_t")
-        ka_t = list_tile(ka, "ka_t")
-        kb_t = list_tile(kb, "kb_t")
         for q in range(4):
-            load_scale_rows(nc.scalar if q < 3 else nc.sync, xs_table, x_scales[0], q)
-        xw_table = keep.tile([P, T], U32, name="xw_table", tag="xw_table", align_bytes=64)
+            rows = w1_scales[0][4 * q : 4 * q + 4, :].bitcast(I32)
+            queue = nc.sync if q < 2 else nc.scalar
+            queue.dma_start(ws_raw[32 * q : 32 * q + 32, :].bitcast(I32), rows.unsqueeze(0).broadcast_to([8, 4, H // 4]))
+        xw_table = keep.tile([P, T], U32, name="xw_table", align_bytes=64)
         nc.scalar.dma_start(xw_table[:].bitcast(I32), x_words[0].rearrange("p n t -> p (n t)").bitcast(I32))
         dw_table = keep.tile([P, G], U32, name="dw_table", align_bytes=64)
         nc.scalar.dma_start(dw_table[:].bitcast(I32), d_words[0].rearrange("p n t -> p (n t)").bitcast(I32))
         for q in range(4):
-            load_scale_rows(nc.sync, ws_raw, w1_scales[0], q)
+            nc.sync.dma_start(xs_table[32 * q : 32 * q + 4, :].bitcast(I32), x_scales[0][4 * q : 4 * q + 4, :].bitcast(I32))
+        ka_t = list_tile(ka, "ka_t")
+        kb_t = list_tile(kb, "kb_t")
         n1_t = list_tile(n1, "n1_t")
         n2_t = list_tile(n2, "n2_t")
         n3_t = list_tile(n3, "n3_t")
         n4_t = list_tile(n4, "n4_t")
         n5_t = list_tile(n5, "n5_t")
 
-        xs = keep.tile([P, S], U8, name="xs", align_bytes=64)
-        nc.vector.tensor_copy(xs[:], xs_table[:].indirect(offs_t[:]))
-
         ww = keep.tile([P, 2 * H], U8, name="ww", align_bytes=64)
+        ws = keep.tile([P, H], U8, name="ws", align_bytes=64)
         nc.scalar.copy(
             ww[:].bitcast(U16).rearrange("p (t m) -> p t m", t=PACK),
             ww_raw[:].bitcast(U16).rearrange("p (m t) -> p t m", t=PACK),
         )
-        ws = keep.tile([P, H], U8, name="ws", align_bytes=64)
         nc.vector.tensor_copy(
             ws[:].rearrange("p (t m) -> p t m", t=PACK), ws_raw[:].rearrange("p (m t) -> p t m", t=PACK)
         )
@@ -110,13 +103,13 @@ def tile_picked_daqunderpagtwo_none_p_kernel(
                 )
             return picked
 
-        ds0 = dictionary_scales(0, "ds_a", "ds_b")
         xw = keep.tile([P, S], U32, name="xw", tag="dw_picked", align_bytes=64)
         nc.vector.tensor_copy(xw[:], xw_table[:].indirect(offs_t[:]))
+        xs = keep.tile([P, S], U8, name="xs", align_bytes=64)
+        nc.vector.tensor_copy(xs[:], xs_table[:].indirect(offs_t[:]))
 
 
-        neg_gs = keep.tile([P, PACK], F32, name="neg_gs")
-        nc.vector.tensor_scalar(neg_gs[:], gs_t[:], -1.0, None, ALU.mult)
+        ds0 = dictionary_scales(0, "ds_a", "ds_b")
 
         y = []
         for t in range(PACK):
@@ -131,7 +124,7 @@ def tile_picked_daqunderpagtwo_none_p_kernel(
                 stop=True,
             )
             y_t = keep.tile([P, S], F32, name=f"y{t}")
-            if t == 0:
+            if t < PACK - 1:
                 nc.scalar.activation(y_t[:], acc[:], COPY)
             else:
                 nc.vector.tensor_copy(y_t[:], acc[:])
@@ -142,23 +135,23 @@ def tile_picked_daqunderpagtwo_none_p_kernel(
 
         def neighbour_step(half, least_tag):
             cols = slice(half * HALF, (half + 1) * HALF)
-            z = keep.tile([P, PACK, HALF], F32, name=f"z{half}")
-            work = keep.tile([P, 2 * PACK, HALF], F32, name=f"work{half}", tag=least_tag, align_bytes=64)
-            least, gy = work[:, :PACK, :], work[:, PACK:, :]
-            for t in range(PACK):
-                at1 = keep.tile([P, HALF], F32, name=f"at1_{half}_{t}")
-                at2 = keep.tile([P, HALF], F32, name=f"at2_{half}_{t}")
-                nc.scalar.activation(at1[:], y[t][:].indirect(entries(n1_t, half * HALF, HALF)), COPY)
-                nc.scalar.activation(at2[:], y[t][:].indirect(entries(n2_t, half * HALF, HALF)), COPY)
-                nc.vector.tensor_scalar(gy[:, t, :], y[t][:, cols], gs_t[:, t : t + 1], None, ALU.mult)
-                nc.vector.tensor_tensor(least[:, t, :], at1[:], at2[:], ALU.min)
-                nc.vector.scalar_tensor_tensor(
-                    z[:, t, :], least[:, t, :], neg_gs[:, t : t + 1], gy[:, t, :], ALU.mult, ALU.add
-                )
+            at1 = keep.tile([P, PACK, HALF], F32, name=f"at1_{half}")
+            at2 = keep.tile([P, PACK, HALF], F32, name=f"at2_{half}")
+            least = keep.tile([P, PACK, HALF], F32, name=f"least{half}", tag=least_tag, align_bytes=64)
+            rise = keep.tile([P, PACK, HALF], F32, name=f"rise{half}")
+            for t0, t1 in ((0, 2), (2, 3), (3, 4)):
+                for t in range(t0, t1):
+                    nc.scalar.activation(at1[:, t, :], y[t][:].indirect(entries(n1_t, half * HALF, HALF)), COPY)
+                    nc.scalar.activation(at2[:, t, :], y[t][:].indirect(entries(n2_t, half * HALF, HALF)), COPY)
+                nc.vector.tensor_tensor(least[:, t0:t1, :], at1[:, t0:t1, :], at2[:, t0:t1, :], ALU.min)
+                for t in range(t0, t1):
+                    nc.vector.tensor_tensor(rise[:, t, :], y[t][:, cols], least[:, t, :], ALU.subtract)
             woven = keep.tile([P, HALF * PACK], BF16, name=f"woven{half}", tag=f"woven{half}", align_bytes=64)
-            nc.vector.tensor_copy(
+            nc.vector.tensor_tensor(
                 woven[:].rearrange("p (c i t) -> p c t i", i=4, t=PACK),
-                z[:].rearrange("p t (c i) -> p c t i", i=4),
+                rise[:].rearrange("p t (c i) -> p c t i", i=4),
+                gs_t[:].unsqueeze(1).unsqueeze(3).broadcast_to([P, HALF // 4, PACK, 4]),
+                ALU.mult,
             )
             nc.vector.quantize_mx(out=z_codes[:, cols].bitcast(FP8X4), scales=z_scales[:, cols], in_=woven[:])
 
@@ -203,10 +196,10 @@ def tile_picked_daqunderpagtwo_none_p_kernel(
         put((0, 1), first_h, 0, HALF)
         second_h = [second_product(dw0, ds0, b, HALF, HALF, 6 + b) for b in (0, 1)]
         put((0, 1), second_h, HALF, HALF)
-        ds1 = dictionary_scales(1, "woven1", "ds_c")
+        ds1 = dictionary_scales(1, "ds_b", "ds_c")
         dw1 = dictionary_words(1)
         last_h = [second_product(dw1, ds1, b, 0, S, b) for b in (2, 3)]
-        take(0, "dw_picked")
+        take(0, "other0")
         take(1, "z_codes")
         put((2, 3), last_h, 0, S)
         take(2, "other2")

@@ -109,8 +109,6 @@ def tile_picked_daqunderpagtwo_none_p_kernel(
         nc.vector.tensor_copy(xs[:], xs_table[:].indirect(offs_t[:]))
 
 
-        ds0 = dictionary_scales(0, "ds_a", "ds_b")
-
         y = []
         for t in range(PACK):
             acc = psum.tile([P, S], F32, name=f"y_acc{t}", tag=f"bank{t}")
@@ -130,6 +128,7 @@ def tile_picked_daqunderpagtwo_none_p_kernel(
                 nc.vector.tensor_copy(y_t[:], acc[:])
             y.append(y_t)
 
+        ds0 = dictionary_scales(0, "ds_a", "ds_b")
         z_codes = keep.tile([P, S], U32, name="z_codes", tag="z_codes", align_bytes=64)
         z_scales = keep.tile([P, S], U8, name="z_scales", align_bytes=64)
 
@@ -138,7 +137,7 @@ def tile_picked_daqunderpagtwo_none_p_kernel(
             at1 = keep.tile([P, PACK, HALF], F32, name=f"at1_{half}")
             at2 = keep.tile([P, PACK, HALF], F32, name=f"at2_{half}")
             least = keep.tile([P, PACK, HALF], F32, name=f"least{half}", tag=least_tag, align_bytes=64)
-            rise = keep.tile([P, PACK, HALF], F32, name=f"rise{half}")
+            rise = keep.tile([P, PACK, HALF], F32, name=f"rise{half}", tag=f"rise{half}", align_bytes=64)
             for t0, t1 in ((0, 2), (2, 3), (3, 4)):
                 for t in range(t0, t1):
                     nc.scalar.activation(at1[:, t, :], y[t][:].indirect(entries(n1_t, half * HALF, HALF)), COPY)
@@ -180,27 +179,28 @@ def tile_picked_daqunderpagtwo_none_p_kernel(
             for b, h in zip(blocks, values):
                 nc.scalar.activation(pages[b][:].indirect(entries(n4_t, first, count)), h[:], COPY, scale=0.5)
 
-        def take(b, tag):
-            other = keep.tile([P, U], F32, name=f"other{b}", tag=tag, align_bytes=64)
-            result = keep.tile([P, U], F32, name=f"result{b}")
-            for c0 in range(0, U, S):
-                cols = slice(c0, c0 + S)
-                nc.scalar.activation(other[:, cols], pages[b][:].indirect(entries(n5_t, c0, S)), COPY)
+        def take(b, tag, widths=(S, S)):
+            other = keep.tile([P, U], F32, name=f"other{b}")
+            result = keep.tile([P, U], F32, name=f"result{b}", tag=tag, align_bytes=64)
+            for i, width in enumerate(widths):
+                c0 = sum(widths[:i])
+                cols = slice(c0, c0 + width)
+                nc.scalar.activation(other[:, cols], pages[b][:].indirect(entries(n5_t, c0, width)), COPY)
                 nc.vector.tensor_tensor(result[:, cols], pages[b][:, cols], other[:, cols], ALU.subtract)
                 nc.sync.dma_start(out[b * P : (b + 1) * P, cols], result[:, cols])
 
         dw0 = dictionary_words(0)
         neighbour_step(0, "least0")
         first_h = [second_product(dw0, ds0, b, 0, HALF, 4 + b) for b in (0, 1)]
-        neighbour_step(1, "woven0")
+        neighbour_step(1, "rise0")
         put((0, 1), first_h, 0, HALF)
         second_h = [second_product(dw0, ds0, b, HALF, HALF, 6 + b) for b in (0, 1)]
         put((0, 1), second_h, HALF, HALF)
         ds1 = dictionary_scales(1, "ds_b", "ds_c")
         dw1 = dictionary_words(1)
         last_h = [second_product(dw1, ds1, b, 0, S, b) for b in (2, 3)]
-        take(0, "other0")
+        take(0, "result0")
         take(1, "z_codes")
         put((2, 3), last_h, 0, S)
-        take(2, "other2")
-        take(3, "other3")
+        take(2, "result2")
+        take(3, "result3", (S, HALF, HALF))

from contextlib import ExitStack

import concourse.mybir as mybir

K, T, S, H, G, U = 512, 2048, 256, 512, 2048, 512
FLOPS = 2 * K * H * S * 3

F32 = mybir.dt.float32
BF16 = mybir.dt.bfloat16
I32 = mybir.dt.int32
U32 = mybir.dt.uint32
U16 = mybir.dt.uint16
U8 = mybir.dt.uint8
FP8X4 = mybir.dt.float8_e4m3fn_x4
FP4X4 = mybir.dt.float4_e2m1fn_x4
ALU = mybir.AluOpType
COPY = mybir.ActivationFunctionType.Copy

P = 128
PACK = 4
HALF = S // 2
PAIR = 2 * P


def entries(offsets, first, count):
    return offsets[:, first // 16 : (first + count) // 16]


def tile_picked_daqunderpagtwo_none_p_kernel(
    tc, x_words, x_scales, w1_words, w1_scales, gs, d_words, d_scales, offs, n1, n2, ka, kb, n3, n4, n5, out
):
    nc = tc.nc
    with ExitStack() as ctx:
        lists = ctx.enter_context(tc.tile_pool(name="lists", bufs=1))
        keep = ctx.enter_context(tc.tile_pool(name="keep", bufs=1))
        psum = ctx.enter_context(tc.psum_pool(name="psum", bufs=1))

        def list_tile(source, name):
            tile = lists.tile([P, source.shape[1]], U16, name=name)
            nc.sync.dma_start(tile[:], source)
            return tile

        xs_table = keep.tile([P, T], U8, name="xs_table", align_bytes=64)
        ws_raw = keep.tile([P, H], U8, name="ws_raw", align_bytes=64)
        ds_table = keep.tile([P, G], U8, name="ds_table", align_bytes=64)
        nc.vector.memset(ds_table[:].bitcast(I32), 0)
        nc.vector.memset(xs_table[:].bitcast(I32), 0)

        ww_raw = keep.tile([P, 2 * H], U8, name="ww_raw", align_bytes=64)
        nc.gpsimd.dma_start(ww_raw[:].bitcast(I32), w1_words[0].bitcast(I32))
        nc.gpsimd.dma_start(ds_table[0:P:8, :].bitcast(I32), d_scales[0].bitcast(I32))
        gs_t = keep.tile([P, PACK], F32, name="gs_t")
        nc.gpsimd.dma_start(gs_t[:], gs.rearrange("(p t) o -> p (t o)", t=PACK))

        offs_t = list_tile(offs, "offs_t")
        for q in range(4):
            rows = w1_scales[0][4 * q : 4 * q + 4, :].bitcast(I32)
            queue = nc.sync if q < 2 else nc.scalar
            queue.dma_start(ws_raw[32 * q : 32 * q + 32, :].bitcast(I32), rows.unsqueeze(0).broadcast_to([8, 4, H // 4]))
        xw_table = keep.tile([P, T], U32, name="xw_table", align_bytes=64)
        nc.scalar.dma_start(xw_table[:].bitcast(I32), x_words[0].rearrange("p n t -> p (n t)").bitcast(I32))
        dw_table = keep.tile([P, G], U32, name="dw_table", align_bytes=64)
        nc.scalar.dma_start(dw_table[:].bitcast(I32), d_words[0].rearrange("p n t -> p (n t)").bitcast(I32))
        for q in range(4):
            nc.sync.dma_start(xs_table[32 * q : 32 * q + 4, :].bitcast(I32), x_scales[0][4 * q : 4 * q + 4, :].bitcast(I32))
        ka_t = list_tile(ka, "ka_t")
        kb_t = list_tile(kb, "kb_t")
        n1_t = list_tile(n1, "n1_t")
        n2_t = list_tile(n2, "n2_t")
        n3_t = list_tile(n3, "n3_t")
        n4_t = list_tile(n4, "n4_t")
        n5_t = list_tile(n5, "n5_t")

        ww = keep.tile([P, 2 * H], U8, name="ww", align_bytes=64)
        ws = keep.tile([P, H], U8, name="ws", align_bytes=64)
        nc.scalar.copy(
            ww[:].bitcast(U16).rearrange("p (t m) -> p t m", t=PACK),
            ww_raw[:].bitcast(U16).rearrange("p (m t) -> p t m", t=PACK),
        )
        nc.vector.tensor_copy(
            ws[:].rearrange("p (t m) -> p t m", t=PACK), ws_raw[:].rearrange("p (m t) -> p t m", t=PACK)
        )

        def dictionary_scales(pair, picked_tag, placed_tag):
            picked = keep.tile([P, 2 * PAIR], U8, name=f"ds_picked{pair}", tag=picked_tag, align_bytes=64)
            for side, codes in enumerate((ka_t, kb_t)):
                nc.vector.tensor_copy(
                    picked[:, side * PAIR : (side + 1) * PAIR],
                    ds_table[:].indirect(entries(codes, pair * PAIR, PAIR)),
                )
            placed = keep.tile([P, 2 * PAIR], U8, name=f"ds_placed{pair}", tag=placed_tag, align_bytes=64)
            nc.vector.memset(placed[:].bitcast(I32), 0)
            for r in range(4):
                nc.sync.dma_start(placed[r:P:32, :].bitcast(I32), picked[8 * r : P : 32, :].bitcast(I32))
            return placed

        def dictionary_words(pair):
            picked = keep.tile([P, 2 * PAIR], U32, name=f"dw_picked{pair}", tag="dw_picked", align_bytes=64)
            for side, codes in enumerate((ka_t, kb_t)):
                nc.vector.tensor_copy(
                    picked[:, side * PAIR : (side + 1) * PAIR],
                    dw_table[:].indirect(entries(codes, pair * PAIR, PAIR)),
                )
            return picked

        xw = keep.tile([P, S], U32, name="xw", tag="dw_picked", align_bytes=64)
        nc.vector.tensor_copy(xw[:], xw_table[:].indirect(offs_t[:]))
        xs = keep.tile([P, S], U8, name="xs", align_bytes=64)
        nc.vector.tensor_copy(xs[:], xs_table[:].indirect(offs_t[:]))


        y = []
        for t in range(PACK):
            acc = psum.tile([P, S], F32, name=f"y_acc{t}", tag=f"bank{t}")
            nc.tensor.matmul_mx(
                out=acc[:],
                lhsT=ww[:, 2 * P * t : 2 * P * (t + 1)].bitcast(FP4X4),
                lhsT_scale=ws[:, P * t : P * (t + 1)],
                rhs=xw[:].bitcast(FP8X4),
                rhs_scale=xs[:],
                start=True,
                stop=True,
            )
            y_t = keep.tile([P, S], F32, name=f"y{t}")
            if t < PACK - 1:
                nc.scalar.activation(y_t[:], acc[:], COPY)
            else:
                nc.vector.tensor_copy(y_t[:], acc[:])
            y.append(y_t)

        ds0 = dictionary_scales(0, "ds_a", "ds_b")
        z_codes = keep.tile([P, S], U32, name="z_codes", tag="z_codes", align_bytes=64)
        z_scales = keep.tile([P, S], U8, name="z_scales", align_bytes=64)

        def neighbour_step(half, least_tag):
            cols = slice(half * HALF, (half + 1) * HALF)
            at1 = keep.tile([P, PACK, HALF], F32, name=f"at1_{half}")
            at2 = keep.tile([P, PACK, HALF], F32, name=f"at2_{half}")
            least = keep.tile([P, PACK, HALF], F32, name=f"least{half}", tag=least_tag, align_bytes=64)
            rise = keep.tile([P, PACK, HALF], F32, name=f"rise{half}", tag=f"rise{half}", align_bytes=64)
            for t0, t1 in ((0, 2), (2, 3), (3, 4)):
                for t in range(t0, t1):
                    nc.scalar.activation(at1[:, t, :], y[t][:].indirect(entries(n1_t, half * HALF, HALF)), COPY)
                    nc.scalar.activation(at2[:, t, :], y[t][:].indirect(entries(n2_t, half * HALF, HALF)), COPY)
                nc.vector.tensor_tensor(least[:, t0:t1, :], at1[:, t0:t1, :], at2[:, t0:t1, :], ALU.min)
                for t in range(t0, t1):
                    nc.vector.tensor_tensor(rise[:, t, :], y[t][:, cols], least[:, t, :], ALU.subtract)
            woven = keep.tile([P, HALF * PACK], BF16, name=f"woven{half}", tag=f"woven{half}", align_bytes=64)
            nc.vector.tensor_tensor(
                woven[:].rearrange("p (c i t) -> p c t i", i=4, t=PACK),
                rise[:].rearrange("p t (c i) -> p c t i", i=4),
                gs_t[:].unsqueeze(1).unsqueeze(3).broadcast_to([P, HALF // 4, PACK, 4]),
                ALU.mult,
            )
            nc.vector.quantize_mx(out=z_codes[:, cols].bitcast(FP8X4), scales=z_scales[:, cols], in_=woven[:])

        def second_product(words, scales, block, first, count, bank):
            acc = psum.tile([P, count], F32, name=f"h_acc{block}_{first}", tag=f"bank{bank}")
            for side in range(2):
                c0 = side * PAIR + (block % 2) * P
                nc.tensor.matmul_mx(
                    out=acc[:],
                    lhsT=words[:, c0 : c0 + P].bitcast(FP8X4),
                    lhsT_scale=scales[:, c0 : c0 + P],
                    rhs=z_codes[:, first : first + count].bitcast(FP8X4),
                    rhs_scale=z_scales[:, first : first + count],
                    start=(side == 0),
                    stop=(side == 1),
                )
            h = keep.tile([P, count], F32, name=f"h{block}_{first}")
            nc.vector.tensor_scalar(h[:], acc[:], 0.0625, None, ALU.mult)
            return h

        pages = [keep.tile([P, U], F32, name=f"page{b}") for b in range(H // P)]

        def put(blocks, values, first, count):
            for b, h in zip(blocks, values):
                nc.scalar.activation(pages[b][:].indirect(entries(n3_t, first, count)), h[:], COPY)
            for b, h in zip(blocks, values):
                nc.scalar.activation(pages[b][:].indirect(entries(n4_t, first, count)), h[:], COPY, scale=0.5)

        def take(b, tag, widths=(S, S)):
            other = keep.tile([P, U], F32, name=f"other{b}")
            result = keep.tile([P, U], F32, name=f"result{b}", tag=tag, align_bytes=64)
            for i, width in enumerate(widths):
                c0 = sum(widths[:i])
                cols = slice(c0, c0 + width)
                nc.scalar.activation(other[:, cols], pages[b][:].indirect(entries(n5_t, c0, width)), COPY)
                nc.vector.tensor_tensor(result[:, cols], pages[b][:, cols], other[:, cols], ALU.subtract)
                nc.sync.dma_start(out[b * P : (b + 1) * P, cols], result[:, cols])

        dw0 = dictionary_words(0)
        neighbour_step(0, "least0")
        first_h = [second_product(dw0, ds0, b, 0, HALF, 4 + b) for b in (0, 1)]
        neighbour_step(1, "rise0")
        put((0, 1), first_h, 0, HALF)
        second_h = [second_product(dw0, ds0, b, HALF, HALF, 6 + b) for b in (0, 1)]
        put((0, 1), second_h, HALF, HALF)
        ds1 = dictionary_scales(1, "ds_b", "ds_c")
        dw1 = dictionary_words(1)
        last_h = [second_product(dw1, ds1, b, 0, S, b) for b in (2, 3)]
        take(0, "result0")
        take(1, "z_codes")
        put((2, 3), last_h, 0, S)
        take(2, "result2")
        take(3, "result3", (S, HALF, HALF))
